import numpy as np
import ml_dtypes


def mxq(x, axis, fmt="e4m3"):
    dtype, down = {"e4m3": (ml_dtypes.float8_e4m3fn, 7), "e5m2": (ml_dtypes.float8_e5m2, 14)}[fmt]
    v = np.moveaxis(np.asarray(x, np.float32).astype(ml_dtypes.bfloat16).astype(np.float64), axis, -1)
    blocks = v.reshape(v.shape[:-1] + (-1, 32))
    amax = np.abs(blocks).max(-1, keepdims=True)
    byte = np.maximum(np.where(amax > 0, np.frexp(amax)[1] - 1 + 127, 0) - down, 1)
    scale = np.exp2(byte - 127.0)
    codes = (blocks / scale).astype(np.float32).astype(dtype).astype(np.float64)
    return np.moveaxis((codes * scale).reshape(v.shape), -1, axis)


WIDE = False


def mx_kscale(k):
    if not WIDE:
        return np.ones(k)
    levels = np.array([30, -30])
    if k % 512:
        return np.exp2(np.random.permutation(np.resize(levels, k // 32))).repeat(32)
    a = np.empty((k // 512, 16))
    for p in range(k // 512):
        a[p, :8] = np.random.permutation(np.resize(levels, 8))
        for g in range(8):
            far = levels[np.abs(levels - a[p, g]) >= 10]
            a[p, g + 8] = far[np.random.randint(len(far))]
    return np.exp2(a.ravel()).repeat(32)


def f64(x):
    return np.asarray(x).astype(np.float64)


def striped(idx):
    return np.tile(np.asarray(idx).reshape(-1, 16).T, (8, 1)).astype(np.uint16)


def unstriped(offs):
    return offs[:16].T.reshape(-1).astype(np.int64)


def striped8(idx):
    return np.asarray(idx).reshape(8, -1, 16).transpose(0, 2, 1).reshape(128, -1).astype(np.uint16)


def unstriped8(offs):
    return offs.reshape(8, 16, -1).transpose(0, 2, 1).reshape(8, -1).astype(np.int64)


def pick8(x, idx, run):
    r = np.arange(len(x))
    return x[r[:, None], idx[r % (8 * run) // run]]


E2M1 = np.array([0.0, 0.5, 1.0, 1.5, 2.0, 3.0, 4.0, 6.0, -0.0, -0.5, -1.0, -1.5, -2.0, -3.0, -4.0, -6.0])


def pack_weight(w, fmt):
    k, n = w.shape
    w = f64(np.asarray(w, np.float32).astype(ml_dtypes.bfloat16)).reshape(k // 32, 32, n)
    amax = np.abs(w).max(1)
    if fmt in ("e4m3", "e5m2"):
        byte = np.frexp(amax)[1] - 1 + 127 - (7 if fmt == "e4m3" else 14)
    else:
        mant, ex = np.frexp(amax / 6.0)
        byte = np.where(mant > 0.5, ex, ex - 1) + 127
    byte = np.clip(np.where(amax > 0, byte, 1), 1, 254)
    scaled = (w * np.exp2(127.0 - byte)[:, None, :]).reshape(k, n).astype(np.float32)
    by_word = np.ascontiguousarray(scaled.reshape(k // 512, 128, 4, n).transpose(0, 1, 3, 2))
    if fmt in ("e4m3", "e5m2"):
        words = by_word.astype(ml_dtypes.float8_e4m3fn if fmt == "e4m3" else ml_dtypes.float8_e5m2).view(np.uint8)
    else:
        c = by_word.astype(ml_dtypes.float4_e2m1fn).view(np.uint8) & 0xF
        words = (c[..., 0::2] | (c[..., 1::2] << 4)).reshape(k // 512, 128, 2 * n)
    return np.ascontiguousarray(words), np.ascontiguousarray(byte.astype(np.uint8).reshape(k // 512, 16, n))


def unpack_weight(words, scales, fmt):
    g, _, n = scales.shape
    words = np.ascontiguousarray(words).reshape(g, 128, n, -1)
    if fmt in ("e4m3", "e5m2"):
        vals = words.view(ml_dtypes.float8_e4m3fn if fmt == "e4m3" else ml_dtypes.float8_e5m2).astype(np.float64)
    else:
        nib = np.empty((g, 128, n, 4), np.uint8)
        nib[..., 0::2] = words & 0xF
        nib[..., 1::2] = words >> 4
        vals = E2M1[nib]
    vals = vals * np.repeat(np.exp2(scales.astype(np.float64) - 127.0), 8, axis=1)[..., None]
    return vals.transpose(0, 1, 3, 2).reshape(g * 512, n)


K, T, J, R, C, O, N, E = 512, 1024, 256, 512, 512, 128, 256, 512


def setup_inputs():
    n = np.random.standard_normal
    idx = np.random.permutation(T)[:J]
    idx2 = np.stack([np.random.permutation(C)[:J] for _ in range(8)])
    idx3 = np.stack([np.random.permutation(C)[:J] for _ in range(8)])
    idx4 = np.random.permutation(C)[:O]
    idx5 = np.random.permutation(C)[:O]
    idx6 = np.stack([np.random.permutation(E)[:O] for _ in range(8)])
    idx7 = np.random.permutation(E)[:O]
    fk = mx_kscale(K)
    fr = mx_kscale(R)
    xtp = pack_weight(n((K, T)) / fk[:, None], "e2m1")
    wp = pack_weight(n((K, R)) * 1 / np.sqrt(K) * fk[:, None] * fr, "e4m3")
    w2p = pack_weight(n((K, R)) * 1 / np.sqrt(K) * fk[:, None] * fr, "e5m2")
    wbp = pack_weight(n((R, N)) * 1 / np.sqrt(R) / fr[:, None], "e2m1")
    return {
        "xt_words": xtp[0],
        "xt_scales": xtp[1],
        "w_words": wp[0],
        "w_scales": wp[1],
        "w2_words": w2p[0],
        "w2_scales": w2p[1],
        "sa": (np.random.uniform(0.5, 1.6, (R, 1))).astype(np.float32),
        "sb": (np.random.uniform(0.5, 1.6, (R, 1))).astype(np.float32),
        "wb_words": wbp[0],
        "wb_scales": wbp[1],
        "offs": striped(idx),
        "offs2": striped8(idx2),
        "offs3": striped8(idx3),
        "offs4": striped(idx4),
        "offs5": striped(idx5),
        "offs6": striped8(idx6),
        "offs7": striped(idx7),
    }


def reference(xt_words, xt_scales, w_words, w_scales, w2_words, w2_scales, sa, sb, wb_words, wb_scales, offs, offs2, offs3, offs4, offs5, offs6, offs7):
    idx = unstriped(offs)
    idx2 = unstriped8(offs2)
    idx3 = unstriped8(offs3)
    idx4 = unstriped(offs4)
    idx5 = unstriped(offs5)
    idx6 = unstriped8(offs6)
    idx7 = unstriped(offs7)
    xtu = unpack_weight(xt_words, xt_scales, "e2m1")
    wu = unpack_weight(w_words, w_scales, "e4m3")
    w2u = unpack_weight(w2_words, w2_scales, "e5m2")
    wbu = unpack_weight(wb_words, wb_scales, "e2m1")
    xtidxg = xtu[:, idx]
    a = wu.T @ xtidxg
    b = w2u.T @ xtidxg
    pw = np.zeros((R, C))
    pw[np.arange(R)[:, None], idx2[np.arange(R) % 512 // 64]] = a
    pv = np.zeros((R, C))
    pv[np.arange(R)[:, None], idx3[np.arange(R) % 512 // 64]] = b
    pg = pw + pv
    hid = np.abs(pg[:, idx4] * f64(sa) - pg[:, idx5] * f64(sb))
    hidq = mxq(hid, 0, "e5m2")
    p = wbu.T @ hidq
    pa = np.zeros((N, E))
    pa[np.arange(N)[:, None], idx6[np.arange(N) % 128 // 16]] = p
    pb = np.zeros((N, E))
    pb[:, idx7] = p
    y = pa + pb
    return y

@@ -1,0 +1,207 @@
+from contextlib import ExitStack
+
+import concourse.mybir as mybir
+
+FLOPS = 301989888
+
+F32 = mybir.dt.float32
+BF16 = mybir.dt.bfloat16
+I32 = mybir.dt.int32
+U16 = mybir.dt.uint16
+U8 = mybir.dt.uint8
+E4M3 = mybir.dt.float8_e4m3fn_x4
+E5M2 = mybir.dt.float8_e5m2_x4
+E2M1 = mybir.dt.float4_e2m1fn_x4
+COPY = mybir.ActivationFunctionType.Copy
+ABS = mybir.ActivationFunctionType.Abs
+ALU = mybir.AluOpType
+
+P = 128
+T, J, R, C, O, N, E = 1024, 256, 512, 512, 128, 256, 512
+PACK = 4
+HALF = J // 2
+
+
+def tile_list_ownsum_twow_one_owntwopages_kernel(
+    tc, xt_words, xt_scales, w_words, w_scales, w2_words, w2_scales, sa, sb, wb_words, wb_scales,
+    offs, offs2, offs3, offs4, offs5, offs6, offs7, out,
+):
+    nc = tc.nc
+    with ExitStack() as ctx:
+        keep = ctx.enter_context(tc.tile_pool(name="keep", bufs=1))
+        psum = ctx.enter_context(tc.psum_pool(name="psum", bufs=1))
+
+        def load_list(src, name):
+            tile = keep.tile(list(src.shape), U16, name=name)
+            nc.sync.dma_start(tile[:], src)
+            return tile
+
+        def zeroed_plane(width, name, tag, engine):
+            plane = keep.tile([P, width], U8, name=name, tag=tag, align_bytes=64)
+            engine.memset(plane[:].bitcast(I32), 0)
+            return plane
+
+        def load_plane(plane, scales):
+            for q in range(4):
+                nc.sync.dma_start(plane[32 * q : 32 * q + 4, :].bitcast(I32), scales[0, 4 * q : 4 * q + 4, :].bitcast(I32))
+
+        def zeroed_page(name, tag):
+            page = keep.tile([P, C], F32, name=name, tag=tag, align_bytes=64)
+            nc.vector.memset(page[:], 0.0)
+            return page
+
+        def load_words(words, name):
+            raw = keep.tile([P, R], I32, name=name, tag=name, align_bytes=64)
+            nc.sync.dma_start(raw[:], words[0].rearrange("p n t -> p (n t)").bitcast(I32))
+            return raw
+
+        xt_plane = zeroed_plane(T, "xt_plane", "xt_plane", nc.vector)
+        w2_plane = zeroed_plane(R, "w2_plane", "w2_plane", nc.gpsimd)
+        w_plane = zeroed_plane(R, "w_plane", "w_plane", nc.gpsimd)
+        pw = [zeroed_page(f"pw{i}", f"pw{i}") for i in range(2)]
+        pv = [zeroed_page(f"pv{i}", f"pv{i}") for i in range(2)]
+
+        l1 = load_list(offs, "l1")
+        w_stage = keep.tile([4, 4, R // 4], I32, name="w_stage")
+        nc.sync.dma_start(w_stage[:], w_scales[0].bitcast(I32).rearrange("(q r) n -> r q n", r=4))
+        xt_table = keep.tile([P, T], U16, name="xt_table", tag="xt_table", align_bytes=64)
+        nc.sync.dma_start(xt_table[:].bitcast(I32), xt_words[0].bitcast(I32))
+        w_raw = load_words(w_words, "w_raw")
+        load_plane(xt_plane, xt_scales)
+        l2 = load_list(offs2, "l2")
+        w2_raw = load_words(w2_words, "w2_raw")
+        load_plane(w2_plane, w2_scales)
+        l3 = load_list(offs3, "l3")
+        l4 = load_list(offs4, "l4")
+        l5 = load_list(offs5, "l5")
+        l6 = load_list(offs6, "l6")
+        l7 = load_list(offs7, "l7")
+
+        for q in range(4):
+            nc.vector.tensor_copy(w_plane[32 * q : 32 * q + 4, :].bitcast(I32), w_stage[:, q, :])
+
+        def deal(src, dtype, run, t0, t1, name, tag):
+            dst = keep.tile([P, t1 - t0, P], dtype, name=name, tag=tag, align_bytes=64)
+            nc.vector.tensor_copy(
+                dst[:].rearrange("p t (c i) -> p c t i", i=run),
+                src[:].rearrange("p (c i t) -> p c t i", i=run, t=PACK)[:, :, t0:t1, :],
+            )
+            return [dst[:, i, :] for i in range(t1 - t0)]
+
+        x_codes = keep.tile([P, J], U16, name="x_codes", align_bytes=64)
+        x_scales = keep.tile([P, J], U8, name="x_scales", align_bytes=64)
+
+        def gather_x(h):
+            cols = slice(h * HALF, (h + 1) * HALF)
+            sl = l1[:, h * HALF // 16 : (h + 1) * HALF // 16]
+            nc.vector.tensor_copy(x_codes[:, cols], xt_table[:].indirect(sl))
+            nc.vector.tensor_copy(x_scales[:, cols], xt_plane[:].indirect(sl))
+
+        banks = 7
+        count = [0]
+
+        def first_stage(codes, scales, fmt, cols, name, on_scalar):
+            width = cols.stop - cols.start
+            acc = psum.tile([P, width], F32, name="acc_" + name, tag=f"bank{count[0] % banks}")
+            count[0] = count[0] + 1
+            nc.tensor.matmul_mx(
+                out=acc[:], lhsT=codes.bitcast(fmt), lhsT_scale=scales,
+                rhs=x_codes[:, cols].bitcast(E2M1), rhs_scale=x_scales[:, cols], start=True, stop=True,
+            )
+            res = keep.tile([P, width], F32, name=name)
+            if on_scalar:
+                nc.scalar.activation(res[:], acc[:], COPY)
+            else:
+                nc.vector.tensor_copy(res[:], acc[:])
+            return res
+
+        w_s = deal(w_plane, U8, 16, 0, 1, "w_s0", "w_s0")
+        gather_x(0)
+        w_c = deal(w_raw, I32, 4, 0, 1, "w_c0", "w_c0")
+        a0_lo = first_stage(w_c[0], w_s[0], E4M3, slice(0, HALF), "a0_lo", True)
+        gather_x(1)
+        a0_hi = first_stage(w_c[0], w_s[0], E4M3, slice(HALF, J), "a0_hi", False)
+        w_s = w_s + deal(w_plane, U8, 16, 1, PACK, "w_s1", "xt_plane")
+        w_c = w_c + deal(w_raw, I32, 4, 1, PACK, "w_c1", "xt_table")
+        every = slice(0, J)
+        a = [None] * PACK
+        b = [None] * PACK
+        a[1] = first_stage(w_c[1], w_s[1], E4M3, every, "a1", False)
+        w2_s = deal(w2_plane, U8, 16, 0, PACK, "w2_s", "w_plane")
+        w2_c = deal(w2_raw, I32, 4, 0, PACK, "w2_c", "w_raw")
+        for t in range(2):
+            b[t] = first_stage(w2_c[t], w2_s[t], E5M2, every, f"b{t}", False)
+        for t in range(2, PACK):
+            a[t] = first_stage(w_c[t], w_s[t], E4M3, every, f"a{t}", False)
+            b[t] = first_stage(w2_c[t], w2_s[t], E5M2, every, f"b{t}", False)
+
+        sa_t = keep.tile([P, PACK], F32, name="sa_t", tag="w_s0", align_bytes=64)
+        nc.sync.dma_start(sa_t[:], sa.rearrange("(p t) o -> p (t o)", t=PACK))
+        sb_t = keep.tile([P, PACK], F32, name="sb_t", tag="w_c0", align_bytes=64)
+        nc.sync.dma_start(sb_t[:], sb.rearrange("(p t) o -> p (t o)", t=PACK))
+        wb_codes = keep.tile([P, 2 * N], U8, name="wb_codes", tag="w2_raw", align_bytes=64)
+        nc.sync.dma_start(wb_codes[:].bitcast(I32), wb_words[0].bitcast(I32))
+        wb_plane = zeroed_plane(N, "wb_plane", "w2_plane", nc.vector)
+        load_plane(wb_plane, wb_scales)
+
+        pg = [keep.tile([P, C], F32, name=f"pg{t}") for t in range(PACK)]
+
+        def put(page, offsets, values):
+            nc.scalar.activation(page[:].indirect(offsets), values[:], COPY)
+
+        def join(t):
+            nc.vector.tensor_tensor(pg[t][:], pw[t % 2][:], pv[t % 2][:], ALU.add)
+
+        put(pw[0], l2[:, 0 : HALF // 16], a0_lo)
+        put(pw[0], l2[:, HALF // 16 : J // 16], a0_hi)
+        put(pw[1], l2[:], a[1])
+        put(pv[0], l3[:], b[0])
+        put(pv[1], l3[:], b[1])
+        join(0)
+        join(1)
+        for t in range(2, PACK):
+            put(pw[t % 2], l2[:], a[t])
+            put(pv[t % 2], l3[:], b[t])
+            join(t)
+
+        pa = [zeroed_page("pa0", "pw0"), zeroed_page("pa1", "w_raw")]
+        pb = [zeroed_page("pb0", "pv0"), zeroed_page("pb1", "xt_table")]
+
+        diff = [keep.tile([P, 2, O], F32, name=f"diff{u}") for u in range(2)]
+        hid = keep.tile([P, O, PACK], BF16, name="hid", align_bytes=64)
+        for t in range(PACK):
+            ga = keep.tile([P, O], F32, name=f"ga{t}")
+            gb = keep.tile([P, O], F32, name=f"gb{t}")
+            nc.scalar.activation(ga[:], pg[t][:].indirect(l4[:]), COPY, scale=sa_t[:, t : t + 1])
+            nc.scalar.activation(gb[:], pg[t][:].indirect(l5[:]), COPY, scale=sb_t[:, t : t + 1])
+            nc.vector.tensor_tensor(diff[t // 2][:, t % 2, :], ga[:], gb[:], ALU.subtract)
+            if t == 1:
+                d = diff[0][:].rearrange("p t o -> p o t")
+                nc.vector.scalar_tensor_tensor(hid[:, :, 0:2], d, -1.0, d, ALU.mult, ALU.max)
+        nc.scalar.activation(hid[:, :, 2:4], diff[1][:].rearrange("p t o -> p o t"), ABS)
+
+        hid_codes = keep.tile([P, O], I32, name="hid_codes", align_bytes=64)
+        hid_scales = keep.tile([P, O], U8, name="hid_scales", align_bytes=64)
+        nc.vector.quantize_mx(out=hid_codes[:].bitcast(E5M2), scales=hid_scales[:], in_=hid[:].rearrange("p o t -> p (o t)"))
+
+        p = []
+        for h in range(2):
+            acc = psum.tile([P, O], F32, name=f"acc_p{h}", tag=f"bank{h}")
+            nc.tensor.matmul_mx(
+                out=acc[:], lhsT=wb_codes[:, 2 * P * h : 2 * P * (h + 1)].bitcast(E2M1),
+                lhsT_scale=wb_plane[:, P * h : P * (h + 1)],
+                rhs=hid_codes[:].bitcast(E5M2), rhs_scale=hid_scales[:], start=True, stop=True,
+            )
+            res = keep.tile([P, O], F32, name=f"p{h}")
+            if h == 0:
+                nc.scalar.activation(res[:], acc[:], COPY)
+            else:
+                nc.vector.tensor_copy(res[:], acc[:])
+            p.append(res)
+        for h in range(2):
+            put(pa[h], l6[:], p[h])
+            nc.vector.tensor_copy(pb[h][:].indirect(l7[:]), p[h][:])
+        for h in range(2):
+            y = keep.tile([P, E], F32, name=f"y{h}")
+            nc.vector.tensor_tensor(y[:], pa[h][:], pb[h][:], ALU.add)
+            nc.sync.dma_start(out[P * h : P * (h + 1), :], y[:])

@@ -41,13 +41,13 @@ def tile_list_ownsum_twow_one_owntwopages_kernel(
             engine.memset(plane[:].bitcast(I32), 0)
             return plane
 
-        def load_plane(plane, scales):
-            for q in range(4):
-                nc.sync.dma_start(plane[32 * q : 32 * q + 4, :].bitcast(I32), scales[0, 4 * q : 4 * q + 4, :].bitcast(I32))
+        def load_plane(queue, plane, scales, quadrants):
+            for q in range(quadrants):
+                queue.dma_start(plane[32 * q : 32 * q + 4, :].bitcast(I32), scales[0, 4 * q : 4 * q + 4, :].bitcast(I32))
 
         def zeroed_page(name, tag):
             page = keep.tile([P, C], F32, name=name, tag=tag, align_bytes=64)
-            nc.vector.memset(page[:], 0.0)
+            nc.vector.memset(page[:].bitcast(I32), 0)
             return page
 
         def load_words(words, name):
@@ -55,36 +55,42 @@ def tile_list_ownsum_twow_one_owntwopages_kernel(
             nc.sync.dma_start(raw[:], words[0].rearrange("p n t -> p (n t)").bitcast(I32))
             return raw
 
-        xt_plane = zeroed_plane(T, "xt_plane", "xt_plane", nc.vector)
-        w2_plane = zeroed_plane(R, "w2_plane", "w2_plane", nc.gpsimd)
-        w_plane = zeroed_plane(R, "w_plane", "w_plane", nc.gpsimd)
-        pw = [zeroed_page(f"pw{i}", f"pw{i}") for i in range(2)]
-        pv = [zeroed_page(f"pv{i}", f"pv{i}") for i in range(2)]
+        def load_stage(scales, name):
+            stage = keep.tile([4, 4, R // 4], I32, name=name, tag=name, align_bytes=64)
+            nc.sync.dma_start(stage[:], scales[0].bitcast(I32).rearrange("(q r) n -> r q n", r=4))
+            return stage
 
+        def spread(plane, stage):
+            for q in range(4):
+                nc.vector.tensor_copy(plane[32 * q : 32 * q + 4, :].bitcast(I32), stage[:, q, :])
+
+        xt_plane = zeroed_plane(T, "xt_plane", "xt_plane", nc.vector)
+        w_plane = zeroed_plane(R, "w_plane", "w_plane", nc.vector)
+        w2_plane = zeroed_plane(R, "w2_plane", "w2_plane", nc.gpsimd)
+        pw = [zeroed_page(f"pw{i}", f"pw{i}") for i in range(PACK - 1)]
+
+        w_stage = load_stage(w_scales, "w_stage")
+        xt_stage = keep.tile([P, 2, T // 4], I32, name="xt_stage")
+        nc.sync.dma_start(xt_stage[64:68], xt_scales[0, 8:16, :].bitcast(I32).rearrange("(q r) n -> r q n", r=4))
         l1 = load_list(offs, "l1")
-        w_stage = keep.tile([4, 4, R // 4], I32, name="w_stage")
-        nc.sync.dma_start(w_stage[:], w_scales[0].bitcast(I32).rearrange("(q r) n -> r q n", r=4))
         xt_table = keep.tile([P, T], U16, name="xt_table", tag="xt_table", align_bytes=64)
         nc.sync.dma_start(xt_table[:].bitcast(I32), xt_words[0].bitcast(I32))
         w_raw = load_words(w_words, "w_raw")
-        load_plane(xt_plane, xt_scales)
         l2 = load_list(offs2, "l2")
+        load_plane(nc.sync, xt_plane, xt_scales, 2)
         w2_raw = load_words(w2_words, "w2_raw")
-        load_plane(w2_plane, w2_scales)
+        load_plane(nc.sync, w2_plane, w2_scales, 4)
         l3 = load_list(offs3, "l3")
         l4 = load_list(offs4, "l4")
         l5 = load_list(offs5, "l5")
         l6 = load_list(offs6, "l6")
         l7 = load_list(offs7, "l7")
 
-        for q in range(4):
-            nc.vector.tensor_copy(w_plane[32 * q : 32 * q + 4, :].bitcast(I32), w_stage[:, q, :])
-
-        def deal(src, dtype, run, t0, t1, name, tag):
+        def deal(engine, src, dtype, run, t0, t1, name, tag):
             dst = keep.tile([P, t1 - t0, P], dtype, name=name, tag=tag, align_bytes=64)
-            nc.vector.tensor_copy(
+            engine.tensor_copy(
                 dst[:].rearrange("p t (c i) -> p c t i", i=run),
-                src[:].rearrange("p (c i t) -> p c t i", i=run, t=PACK)[:, :, t0:t1, :],
+                src.rearrange("p (c i t) -> p c t i", i=run, t=PACK)[:, :, t0:t1, :],
             )
             return [dst[:, i, :] for i in range(t1 - t0)]
 
@@ -115,57 +121,56 @@ def tile_list_ownsum_twow_one_owntwopages_kernel(
                 nc.vector.tensor_copy(res[:], acc[:])
             return res
 
-        w_s = deal(w_plane, U8, 16, 0, 1, "w_s0", "w_s0")
+        spread(w_plane, w_stage)
+        for q in range(2, 4):
+            nc.vector.tensor_copy(xt_plane[32 * q : 32 * q + 4, :].bitcast(I32), xt_stage[64:68, q - 2, :])
+        w_s = deal(nc.vector, w_plane[:], U8, 16, 0, 1, "w_s0", "w_s0")
         gather_x(0)
-        w_c = deal(w_raw, I32, 4, 0, 1, "w_c0", "w_c0")
+        w_c = deal(nc.vector, w_raw[:], I32, 4, 0, 1, "w_c0", "w_c0")
         a0_lo = first_stage(w_c[0], w_s[0], E4M3, slice(0, HALF), "a0_lo", True)
         gather_x(1)
         a0_hi = first_stage(w_c[0], w_s[0], E4M3, slice(HALF, J), "a0_hi", False)
-        w_s = w_s + deal(w_plane, U8, 16, 1, PACK, "w_s1", "xt_plane")
-        w_c = w_c + deal(w_raw, I32, 4, 1, PACK, "w_c1", "xt_table")
+        w_s = w_s + deal(nc.vector, w_plane[:], U8, 16, 1, PACK, "w_s1", "xt_plane")
+        w_c = w_c + deal(nc.vector, w_raw[:], I32, 4, 1, PACK, "w_c1", "xt_table")
         every = slice(0, J)
         a = [None] * PACK
         b = [None] * PACK
-        a[1] = first_stage(w_c[1], w_s[1], E4M3, every, "a1", False)
-        w2_s = deal(w2_plane, U8, 16, 0, PACK, "w2_s", "w_plane")
-        w2_c = deal(w2_raw, I32, 4, 0, PACK, "w2_c", "w_raw")
-        for t in range(2):
-            b[t] = first_stage(w2_c[t], w2_s[t], E5M2, every, f"b{t}", False)
-        for t in range(2, PACK):
+        for t in range(1, PACK):
             a[t] = first_stage(w_c[t], w_s[t], E4M3, every, f"a{t}", False)
+        pw.append(zeroed_page("pw3", "xt_plane"))
+        w2_s = deal(nc.vector, w2_plane[:], U8, 16, 0, PACK, "w2_s", "w_plane")
+        w2_c = deal(nc.vector, w2_raw[:], I32, 4, 0, PACK, "w2_c", "w_raw")
+        for t in range(PACK):
             b[t] = first_stage(w2_c[t], w2_s[t], E5M2, every, f"b{t}", False)
 
         sa_t = keep.tile([P, PACK], F32, name="sa_t", tag="w_s0", align_bytes=64)
-        nc.sync.dma_start(sa_t[:], sa.rearrange("(p t) o -> p (t o)", t=PACK))
+        nc.gpsimd.dma_start(sa_t[:], sa.rearrange("(p t) o -> p (t o)", t=PACK))
         sb_t = keep.tile([P, PACK], F32, name="sb_t", tag="w_c0", align_bytes=64)
-        nc.sync.dma_start(sb_t[:], sb.rearrange("(p t) o -> p (t o)", t=PACK))
-        wb_codes = keep.tile([P, 2 * N], U8, name="wb_codes", tag="w2_raw", align_bytes=64)
-        nc.sync.dma_start(wb_codes[:].bitcast(I32), wb_words[0].bitcast(I32))
-        wb_plane = zeroed_plane(N, "wb_plane", "w2_plane", nc.vector)
-        load_plane(wb_plane, wb_scales)
+        nc.gpsimd.dma_start(sb_t[:], sb.rearrange("(p t) o -> p (t o)", t=PACK))
+        wb_codes = keep.tile([P, 2 * N], U8, name="wb_codes", tag="w_plane", align_bytes=64)
+        nc.gpsimd.dma_start(wb_codes[:].bitcast(I32), wb_words[0].bitcast(I32))
+        wb_plane = zeroed_plane(N, "wb_plane", "w2_plane", nc.gpsimd)
+        load_plane(nc.gpsimd, wb_plane, wb_scales, 4)
 
+        pv = [zeroed_page("pv0", "xt_table"), zeroed_page("pv1", "w2_raw")]
         pg = [keep.tile([P, C], F32, name=f"pg{t}") for t in range(PACK)]
 
         def put(page, offsets, values):
             nc.scalar.activation(page[:].indirect(offsets), values[:], COPY)
 
         def join(t):
-            nc.vector.tensor_tensor(pg[t][:], pw[t % 2][:], pv[t % 2][:], ALU.add)
+            nc.vector.tensor_tensor(pg[t][:], pw[t][:], pv[t % 2][:], ALU.add)
 
         put(pw[0], l2[:, 0 : HALF // 16], a0_lo)
         put(pw[0], l2[:, HALF // 16 : J // 16], a0_hi)
-        put(pw[1], l2[:], a[1])
-        put(pv[0], l3[:], b[0])
-        put(pv[1], l3[:], b[1])
-        join(0)
-        join(1)
-        for t in range(2, PACK):
-            put(pw[t % 2], l2[:], a[t])
+        for t in range(1, PACK):
+            put(pw[t], l2[:], a[t])
+        for t in range(PACK):
             put(pv[t % 2], l3[:], b[t])
             join(t)
 
         pa = [zeroed_page("pa0", "pw0"), zeroed_page("pa1", "w_raw")]
-        pb = [zeroed_page("pb0", "pv0"), zeroed_page("pb1", "xt_table")]
+        pb = [zeroed_page("pb0", "pw1"), zeroed_page("pb1", "pw2")]
 
         diff = [keep.tile([P, 2, O], F32, name=f"diff{u}") for u in range(2)]
         hid = keep.tile([P, O, PACK], BF16, name="hid", align_bytes=64)

@@ -7,6 +7,7 @@ FLOPS = 301989888
 F32 = mybir.dt.float32
 BF16 = mybir.dt.bfloat16
 I32 = mybir.dt.int32
+U32 = mybir.dt.uint32
 U16 = mybir.dt.uint16
 U8 = mybir.dt.uint8
 E4M3 = mybir.dt.float8_e4m3fn_x4
@@ -45,9 +46,9 @@ def tile_list_ownsum_twow_one_owntwopages_kernel(
             for q in range(quadrants):
                 queue.dma_start(plane[32 * q : 32 * q + 4, :].bitcast(I32), scales[0, 4 * q : 4 * q + 4, :].bitcast(I32))
 
-        def zeroed_page(name, tag):
+        def zeroed_page(name, tag, engine=nc.vector):
             page = keep.tile([P, C], F32, name=name, tag=tag, align_bytes=64)
-            nc.vector.memset(page[:].bitcast(I32), 0)
+            engine.memset(page[:].bitcast(I32), 0)
             return page
 
         def load_words(words, name):
@@ -67,7 +68,7 @@ def tile_list_ownsum_twow_one_owntwopages_kernel(
         xt_plane = zeroed_plane(T, "xt_plane", "xt_plane", nc.vector)
         w_plane = zeroed_plane(R, "w_plane", "w_plane", nc.vector)
         w2_plane = zeroed_plane(R, "w2_plane", "w2_plane", nc.gpsimd)
-        pw = [zeroed_page(f"pw{i}", f"pw{i}") for i in range(PACK - 1)]
+        pw = [zeroed_page(f"pw{i}", f"pw{i}", nc.vector if i < PACK - 1 else nc.gpsimd) for i in range(PACK)]
 
         w_stage = load_stage(w_scales, "w_stage")
         xt_stage = keep.tile([P, 2, T // 4], I32, name="xt_stage")
@@ -86,9 +87,9 @@ def tile_list_ownsum_twow_one_owntwopages_kernel(
         l6 = load_list(offs6, "l6")
         l7 = load_list(offs7, "l7")
 
-        def deal(engine, src, dtype, run, t0, t1, name, tag):
+        def deal(copy, src, dtype, run, t0, t1, name, tag):
             dst = keep.tile([P, t1 - t0, P], dtype, name=name, tag=tag, align_bytes=64)
-            engine.tensor_copy(
+            copy(
                 dst[:].rearrange("p t (c i) -> p c t i", i=run),
                 src.rearrange("p (c i t) -> p c t i", i=run, t=PACK)[:, :, t0:t1, :],
             )
@@ -114,7 +115,7 @@ def tile_list_ownsum_twow_one_owntwopages_kernel(
                 out=acc[:], lhsT=codes.bitcast(fmt), lhsT_scale=scales,
                 rhs=x_codes[:, cols].bitcast(E2M1), rhs_scale=x_scales[:, cols], start=True, stop=True,
             )
-            res = keep.tile([P, width], F32, name=name)
+            res = keep.tile([P, width], F32, name=name, tag=name, align_bytes=64)
             if on_scalar:
                 nc.scalar.activation(res[:], acc[:], COPY)
             else:
@@ -124,35 +125,30 @@ def tile_list_ownsum_twow_one_owntwopages_kernel(
         spread(w_plane, w_stage)
         for q in range(2, 4):
             nc.vector.tensor_copy(xt_plane[32 * q : 32 * q + 4, :].bitcast(I32), xt_stage[64:68, q - 2, :])
-        w_s = deal(nc.vector, w_plane[:], U8, 16, 0, 1, "w_s0", "w_s0")
+        w_s = deal(nc.vector.tensor_copy, w_plane[:], U8, 16, 0, 1, "w_s0", "w_s0")
         gather_x(0)
-        w_c = deal(nc.vector, w_raw[:], I32, 4, 0, 1, "w_c0", "w_c0")
+        w_c = deal(nc.scalar.copy, w_raw[:].bitcast(U32), U32, 4, 0, 1, "w_c0", "w_c0")
         a0_lo = first_stage(w_c[0], w_s[0], E4M3, slice(0, HALF), "a0_lo", True)
         gather_x(1)
         a0_hi = first_stage(w_c[0], w_s[0], E4M3, slice(HALF, J), "a0_hi", False)
-        w_s = w_s + deal(nc.vector, w_plane[:], U8, 16, 1, PACK, "w_s1", "xt_plane")
-        w_c = w_c + deal(nc.vector, w_raw[:], I32, 4, 1, PACK, "w_c1", "xt_table")
+        w_s = w_s + deal(nc.vector.tensor_copy, w_plane[:], U8, 16, 1, PACK, "w_s1", "xt_plane")
+        w_c = w_c + deal(nc.scalar.copy, w_raw[:].bitcast(U32), U32, 4, 1, PACK, "w_c1", "w_c1")
         every = slice(0, J)
         a = [None] * PACK
         b = [None] * PACK
         for t in range(1, PACK):
             a[t] = first_stage(w_c[t], w_s[t], E4M3, every, f"a{t}", False)
-        pw.append(zeroed_page("pw3", "xt_plane"))
-        w2_s = deal(nc.vector, w2_plane[:], U8, 16, 0, PACK, "w2_s", "w_plane")
-        w2_c = deal(nc.vector, w2_raw[:], I32, 4, 0, PACK, "w2_c", "w_raw")
+        w2_s = deal(nc.vector.tensor_copy, w2_plane[:], U8, 16, 0, PACK, "w2_s", "xt_plane")
+        w2_c = deal(nc.vector.tensor_copy, w2_raw[:], I32, 4, 0, PACK, "w2_c", "w_c1")
         for t in range(PACK):
             b[t] = first_stage(w2_c[t], w2_s[t], E5M2, every, f"b{t}", False)
 
-        sa_t = keep.tile([P, PACK], F32, name="sa_t", tag="w_s0", align_bytes=64)
-        nc.gpsimd.dma_start(sa_t[:], sa.rearrange("(p t) o -> p (t o)", t=PACK))
-        sb_t = keep.tile([P, PACK], F32, name="sb_t", tag="w_c0", align_bytes=64)
-        nc.gpsimd.dma_start(sb_t[:], sb.rearrange("(p t) o -> p (t o)", t=PACK))
-        wb_codes = keep.tile([P, 2 * N], U8, name="wb_codes", tag="w_plane", align_bytes=64)
-        nc.gpsimd.dma_start(wb_codes[:].bitcast(I32), wb_words[0].bitcast(I32))
-        wb_plane = zeroed_plane(N, "wb_plane", "w2_plane", nc.gpsimd)
-        load_plane(nc.gpsimd, wb_plane, wb_scales, 4)
+        wb_codes = keep.tile([P, 2 * N], U8, name="wb_codes", tag="w_c1", align_bytes=64)
+        nc.sync.dma_start(wb_codes[:].bitcast(I32), wb_words[0].bitcast(I32))
+        wb_plane = zeroed_plane(N, "wb_plane", "xt_plane", nc.vector)
+        load_plane(nc.sync, wb_plane, wb_scales, 4)
 
-        pv = [zeroed_page("pv0", "xt_table"), zeroed_page("pv1", "w2_raw")]
+        pv = [zeroed_page("pv0", "w2_raw"), zeroed_page("pv1", "w2_plane")]
         pg = [keep.tile([P, C], F32, name=f"pg{t}") for t in range(PACK)]
 
         def put(page, offsets, values):
@@ -163,13 +159,17 @@ def tile_list_ownsum_twow_one_owntwopages_kernel(
 
         put(pw[0], l2[:, 0 : HALF // 16], a0_lo)
         put(pw[0], l2[:, HALF // 16 : J // 16], a0_hi)
+        sa_t = keep.tile([P, PACK], F32, name="sa_t", tag="a0_lo", align_bytes=64)
+        nc.sync.dma_start(sa_t[:], sa.rearrange("(p t) o -> p (t o)", t=PACK))
+        sb_t = keep.tile([P, PACK], F32, name="sb_t", tag="a0_hi", align_bytes=64)
+        nc.sync.dma_start(sb_t[:], sb.rearrange("(p t) o -> p (t o)", t=PACK))
         for t in range(1, PACK):
             put(pw[t], l2[:], a[t])
         for t in range(PACK):
             put(pv[t % 2], l3[:], b[t])
             join(t)
 
-        pa = [zeroed_page("pa0", "pw0"), zeroed_page("pa1", "w_raw")]
+        pa = [zeroed_page("pa0", "pw0"), zeroed_page("pa1", "b0")]
         pb = [zeroed_page("pb0", "pw1"), zeroed_page("pb1", "pw2")]
 
         diff = [keep.tile([P, 2, O], F32, name=f"diff{u}") for u in range(2)]

from contextlib import ExitStack

import concourse.mybir as mybir

FLOPS = 301989888

F32 = mybir.dt.float32
BF16 = mybir.dt.bfloat16
I32 = mybir.dt.int32
U32 = mybir.dt.uint32
U16 = mybir.dt.uint16
U8 = mybir.dt.uint8
E4M3 = mybir.dt.float8_e4m3fn_x4
E5M2 = mybir.dt.float8_e5m2_x4
E2M1 = mybir.dt.float4_e2m1fn_x4
COPY = mybir.ActivationFunctionType.Copy
ABS = mybir.ActivationFunctionType.Abs
ALU = mybir.AluOpType

P = 128
T, J, R, C, O, N, E = 1024, 256, 512, 512, 128, 256, 512
PACK = 4
HALF = J // 2


def tile_list_ownsum_twow_one_owntwopages_kernel(
    tc, xt_words, xt_scales, w_words, w_scales, w2_words, w2_scales, sa, sb, wb_words, wb_scales,
    offs, offs2, offs3, offs4, offs5, offs6, offs7, out,
):
    nc = tc.nc
    with ExitStack() as ctx:
        keep = ctx.enter_context(tc.tile_pool(name="keep", bufs=1))
        psum = ctx.enter_context(tc.psum_pool(name="psum", bufs=1))

        def load_list(src, name):
            tile = keep.tile(list(src.shape), U16, name=name)
            nc.sync.dma_start(tile[:], src)
            return tile

        def zeroed_plane(width, name, tag, engine):
            plane = keep.tile([P, width], U8, name=name, tag=tag, align_bytes=64)
            engine.memset(plane[:].bitcast(I32), 0)
            return plane

        def load_plane(queue, plane, scales, quadrants):
            for q in range(quadrants):
                queue.dma_start(plane[32 * q : 32 * q + 4, :].bitcast(I32), scales[0, 4 * q : 4 * q + 4, :].bitcast(I32))

        def zeroed_page(name, tag, engine=nc.vector):
            page = keep.tile([P, C], F32, name=name, tag=tag, align_bytes=64)
            engine.memset(page[:].bitcast(I32), 0)
            return page

        def load_words(words, name):
            raw = keep.tile([P, R], I32, name=name, tag=name, align_bytes=64)
            nc.sync.dma_start(raw[:], words[0].rearrange("p n t -> p (n t)").bitcast(I32))
            return raw

        def load_stage(scales, name):
            stage = keep.tile([4, 4, R // 4], I32, name=name, tag=name, align_bytes=64)
            nc.sync.dma_start(stage[:], scales[0].bitcast(I32).rearrange("(q r) n -> r q n", r=4))
            return stage

        def spread(plane, stage):
            for q in range(4):
                nc.vector.tensor_copy(plane[32 * q : 32 * q + 4, :].bitcast(I32), stage[:, q, :])

        xt_plane = zeroed_plane(T, "xt_plane", "xt_plane", nc.vector)
        w_plane = zeroed_plane(R, "w_plane", "w_plane", nc.vector)
        w2_plane = zeroed_plane(R, "w2_plane", "w2_plane", nc.gpsimd)
        pw = [zeroed_page(f"pw{i}", f"pw{i}", nc.vector if i < PACK - 1 else nc.gpsimd) for i in range(PACK)]

        w_stage = load_stage(w_scales, "w_stage")
        xt_stage = keep.tile([P, 2, T // 4], I32, name="xt_stage")
        nc.sync.dma_start(xt_stage[64:68], xt_scales[0, 8:16, :].bitcast(I32).rearrange("(q r) n -> r q n", r=4))
        l1 = load_list(offs, "l1")
        xt_table = keep.tile([P, T], U16, name="xt_table", tag="xt_table", align_bytes=64)
        nc.sync.dma_start(xt_table[:].bitcast(I32), xt_words[0].bitcast(I32))
        w_raw = load_words(w_words, "w_raw")
        l2 = load_list(offs2, "l2")
        load_plane(nc.sync, xt_plane, xt_scales, 2)
        w2_raw = load_words(w2_words, "w2_raw")
        load_plane(nc.sync, w2_plane, w2_scales, 4)
        l3 = load_list(offs3, "l3")
        l4 = load_list(offs4, "l4")
        l5 = load_list(offs5, "l5")
        l6 = load_list(offs6, "l6")
        l7 = load_list(offs7, "l7")

        def deal(copy, src, dtype, run, t0, t1, name, tag):
            dst = keep.tile([P, t1 - t0, P], dtype, name=name, tag=tag, align_bytes=64)
            copy(
                dst[:].rearrange("p t (c i) -> p c t i", i=run),
                src.rearrange("p (c i t) -> p c t i", i=run, t=PACK)[:, :, t0:t1, :],
            )
            return [dst[:, i, :] for i in range(t1 - t0)]

        x_codes = keep.tile([P, J], U16, name="x_codes", align_bytes=64)
        x_scales = keep.tile([P, J], U8, name="x_scales", align_bytes=64)

        def gather_x(h):
            cols = slice(h * HALF, (h + 1) * HALF)
            sl = l1[:, h * HALF // 16 : (h + 1) * HALF // 16]
            nc.vector.tensor_copy(x_codes[:, cols], xt_table[:].indirect(sl))
            nc.vector.tensor_copy(x_scales[:, cols], xt_plane[:].indirect(sl))

        banks = 7
        count = [0]

        def first_stage(codes, scales, fmt, cols, name, on_scalar):
            width = cols.stop - cols.start
            acc = psum.tile([P, width], F32, name="acc_" + name, tag=f"bank{count[0] % banks}")
            count[0] = count[0] + 1
            nc.tensor.matmul_mx(
                out=acc[:], lhsT=codes.bitcast(fmt), lhsT_scale=scales,
                rhs=x_codes[:, cols].bitcast(E2M1), rhs_scale=x_scales[:, cols], start=True, stop=True,
            )
            res = keep.tile([P, width], F32, name=name, tag=name, align_bytes=64)
            if on_scalar:
                nc.scalar.activation(res[:], acc[:], COPY)
            else:
                nc.vector.tensor_copy(res[:], acc[:])
            return res

        spread(w_plane, w_stage)
        for q in range(2, 4):
            nc.vector.tensor_copy(xt_plane[32 * q : 32 * q + 4, :].bitcast(I32), xt_stage[64:68, q - 2, :])
        w_s = deal(nc.vector.tensor_copy, w_plane[:], U8, 16, 0, 1, "w_s0", "w_s0")
        gather_x(0)
        w_c = deal(nc.scalar.copy, w_raw[:].bitcast(U32), U32, 4, 0, 1, "w_c0", "w_c0")
        a0_lo = first_stage(w_c[0], w_s[0], E4M3, slice(0, HALF), "a0_lo", True)
        gather_x(1)
        a0_hi = first_stage(w_c[0], w_s[0], E4M3, slice(HALF, J), "a0_hi", False)
        w_s = w_s + deal(nc.vector.tensor_copy, w_plane[:], U8, 16, 1, PACK, "w_s1", "xt_plane")
        w_c = w_c + deal(nc.scalar.copy, w_raw[:].bitcast(U32), U32, 4, 1, PACK, "w_c1", "w_c1")
        every = slice(0, J)
        a = [None] * PACK
        b = [None] * PACK
        for t in range(1, PACK):
            a[t] = first_stage(w_c[t], w_s[t], E4M3, every, f"a{t}", False)
        w2_s = deal(nc.vector.tensor_copy, w2_plane[:], U8, 16, 0, PACK, "w2_s", "xt_plane")
        w2_c = deal(nc.vector.tensor_copy, w2_raw[:], I32, 4, 0, PACK, "w2_c", "w_c1")
        for t in range(PACK):
            b[t] = first_stage(w2_c[t], w2_s[t], E5M2, every, f"b{t}", False)

        wb_codes = keep.tile([P, 2 * N], U8, name="wb_codes", tag="w_c1", align_bytes=64)
        nc.sync.dma_start(wb_codes[:].bitcast(I32), wb_words[0].bitcast(I32))
        wb_plane = zeroed_plane(N, "wb_plane", "xt_plane", nc.vector)
        load_plane(nc.sync, wb_plane, wb_scales, 4)

        pv = [zeroed_page("pv0", "w2_raw"), zeroed_page("pv1", "w2_plane")]
        pg = [keep.tile([P, C], F32, name=f"pg{t}") for t in range(PACK)]

        def put(page, offsets, values):
            nc.scalar.activation(page[:].indirect(offsets), values[:], COPY)

        def join(t):
            nc.vector.tensor_tensor(pg[t][:], pw[t][:], pv[t % 2][:], ALU.add)

        put(pw[0], l2[:, 0 : HALF // 16], a0_lo)
        put(pw[0], l2[:, HALF // 16 : J // 16], a0_hi)
        sa_t = keep.tile([P, PACK], F32, name="sa_t", tag="a0_lo", align_bytes=64)
        nc.sync.dma_start(sa_t[:], sa.rearrange("(p t) o -> p (t o)", t=PACK))
        sb_t = keep.tile([P, PACK], F32, name="sb_t", tag="a0_hi", align_bytes=64)
        nc.sync.dma_start(sb_t[:], sb.rearrange("(p t) o -> p (t o)", t=PACK))
        for t in range(1, PACK):
            put(pw[t], l2[:], a[t])
        for t in range(PACK):
            put(pv[t % 2], l3[:], b[t])
            join(t)

        pa = [zeroed_page("pa0", "pw0"), zeroed_page("pa1", "b0")]
        pb = [zeroed_page("pb0", "pw1"), zeroed_page("pb1", "pw2")]

        diff = [keep.tile([P, 2, O], F32, name=f"diff{u}") for u in range(2)]
        hid = keep.tile([P, O, PACK], BF16, name="hid", align_bytes=64)
        for t in range(PACK):
            ga = keep.tile([P, O], F32, name=f"ga{t}")
            gb = keep.tile([P, O], F32, name=f"gb{t}")
            nc.scalar.activation(ga[:], pg[t][:].indirect(l4[:]), COPY, scale=sa_t[:, t : t + 1])
            nc.scalar.activation(gb[:], pg[t][:].indirect(l5[:]), COPY, scale=sb_t[:, t : t + 1])
            nc.vector.tensor_tensor(diff[t // 2][:, t % 2, :], ga[:], gb[:], ALU.subtract)
            if t == 1:
                d = diff[0][:].rearrange("p t o -> p o t")
                nc.vector.scalar_tensor_tensor(hid[:, :, 0:2], d, -1.0, d, ALU.mult, ALU.max)
        nc.scalar.activation(hid[:, :, 2:4], diff[1][:].rearrange("p t o -> p o t"), ABS)

        hid_codes = keep.tile([P, O], I32, name="hid_codes", align_bytes=64)
        hid_scales = keep.tile([P, O], U8, name="hid_scales", align_bytes=64)
        nc.vector.quantize_mx(out=hid_codes[:].bitcast(E5M2), scales=hid_scales[:], in_=hid[:].rearrange("p o t -> p (o t)"))

        p = []
        for h in range(2):
            acc = psum.tile([P, O], F32, name=f"acc_p{h}", tag=f"bank{h}")
            nc.tensor.matmul_mx(
                out=acc[:], lhsT=wb_codes[:, 2 * P * h : 2 * P * (h + 1)].bitcast(E2M1),
                lhsT_scale=wb_plane[:, P * h : P * (h + 1)],
                rhs=hid_codes[:].bitcast(E5M2), rhs_scale=hid_scales[:], start=True, stop=True,
            )
            res = keep.tile([P, O], F32, name=f"p{h}")
            if h == 0:
                nc.scalar.activation(res[:], acc[:], COPY)
            else:
                nc.vector.tensor_copy(res[:], acc[:])
            p.append(res)
        for h in range(2):
            put(pa[h], l6[:], p[h])
            nc.vector.tensor_copy(pb[h][:].indirect(l7[:]), p[h][:])
        for h in range(2):
            y = keep.tile([P, E], F32, name=f"y{h}")
            nc.vector.tensor_tensor(y[:], pa[h][:], pb[h][:], ALU.add)
            nc.sync.dma_start(out[P * h : P * (h + 1), :], y[:])
